import numpy as np, ml_dtypes
CORES = [65,73,81,89,97,105,113,121]
N = 8
import mx_ref
NC, KB = 128, 1
BF = ml_dtypes.bfloat16
def cut(t, i, w=512):
    return t[:, w * i:w * i + w]
def term(a, B):
    return np.stack([mx_ref.matmul(mx_ref.quantize(cut(a, i)), B) for i in range(4)], axis=2).reshape(128, -1)
def setup_inputs(rng):
    def f(*shape):
        return mx_ref.flush((rng.standard_normal(shape, dtype=np.float32) * np.exp2(rng.integers(-2, 3, shape[:-1] + (1,)))).astype(BF))
    return {"a": f(N, 128, 4 * 512), "b": f(N, 128, KB * 4 * NC)}
def setup_inputs_blocks(rng):
    d = setup_inputs(rng)
    for k in ("a", "b"): d[k] = mx_ref.spread(d[k], rng, 2)
    return d
def setup_inputs_wide(rng):
    d = setup_inputs(rng)
    for k in ("a", "b"): d[k] = mx_ref.flush((d[k].astype(np.float32) * np.exp2(rng.integers(-4, 5, (N, 1, 1))).astype(np.float32)).astype(BF))
    return d
def setup_inputs_lossless(rng):
    a = np.zeros((N, 128, 4 * 128, 4), np.float32)
    for r in range(N):
        k = rng.integers(0, 512, size=4 * 128)
        a[r, k // 4, np.arange(4 * 128), k % 4] = 1.0
    size = np.repeat(2.0 ** rng.integers(-4, 5, size=(1, 1, (KB * 4 * NC) // 4)), 4, axis=2)
    b = rng.integers(-1, 2, size=(N, 128, KB * 4 * NC)) * size
    return {"a": a.reshape(N, 128, 4 * 512).astype(BF), "b": b.astype(np.float32).astype(BF)}
def reference(a, b):
    y = np.zeros((N, 128, KB * 4 * NC), np.float32)
    for k in range(KB):
        y[:, :, 4 * NC * k:4 * NC * k + 4 * NC] = mx_ref.total([term(a[r], mx_ref.quantize(cut(b[r], k, 4 * NC))) for r in range(N)])
    return {"y": y}

@@ -1,0 +1,195 @@
+from concourse.bass import DstId, RemoteDMATransfer
+from concourse.mybir import dt, AluOpType, ActivationFunctionType
+
+N = 8
+SIM_CORES = 128
+
+SCRATCH = {
+    "a_sb": ("sbuf", [128, 2048], "bfloat16"),
+    "b_sb": ("sbuf", [128, 512], "bfloat16"),
+    "aq": ("sbuf", [128, 512], "float8_e4m3fn_x4"),
+    "ap": ("sbuf", [128, 512], "uint8"),
+    "bq": ("sbuf", [128, 128], "float8_e4m3fn_x4"),
+    "bp": ("sbuf", [128, 128], "uint8"),
+    "eye": ("sbuf", [128, 128], "bfloat16"),
+    "diag": ("sbuf", [128, 516], "bfloat16"),
+    "wq": ("sbuf", [128, 512], "float8_e4m3fn_x4"),
+    "wp": ("sbuf", [128, 512], "uint8"),
+    "h_sb": ("sbuf", [128, 512], "bfloat16"),
+    "q": ("sbuf", [128, 128], "float8_e4m3fn_x4"),
+    "qp": ("sbuf", [128, 128], "uint8"),
+    "rq": ("sbuf", [128, 128 * N], "float8_e4m3fn_x4"),
+    "rp": ("sbuf", [128, 128 * N], "uint8"),
+    "own": ("psum", [128, 2048], "float32"),
+    "acc": ("psum", [128, 2048], "float32"),
+    "y_sb": ("sbuf", [128, 512], "float32"),
+}
+SEMAPHORES = ["ld_b", "ld_a0", "ld_a1", "c_ones", "c_zero", "c_eye", "c_diag", "w_done", "qb", "qa", "mm",
+              "hcp_v", "hcp_s", "q_done", "feed", "sent", "fin", "ycp_v", "ycp_s", "stored"] + ["arr%d" % s for s in range(N)]
+
+TAKE = ["P1", "P2", "P3", "M", "F2", "F1", "F3"]
+
+
+def _rot(lst, x):
+    k = lst.index(x)
+    return lst[k + 1:] + lst[:k]
+
+
+def _plan(r, cores, topo):
+    me = cores[r]
+    ch = [topo.chip(c) for c in cores]
+    plane = [s for s in range(N) if s == r or topo.same_plane(ch[s], ch[r])]
+    mate = [s for s in range(N) if topo.mates(ch[s], ch[r])][0]
+    other = [s for s in range(N) if s == mate or topo.same_plane(ch[s], ch[mate])]
+    p = _rot(plane, r)
+    f = _rot(other, mate)
+    kinds = {"P1": p[0], "P2": p[1], "P3": p[2], "M": mate, "F1": f[0], "F2": f[1], "F3": f[2]}
+    here = [c for c in range(SIM_CORES) if topo.chip(c) == ch[r] and c != me]
+    gate = [c for c in here if topo.may_write(c, cores[mate])]
+    near = [c for c in gate if topo.die(c) == topo.die(me)]
+    far = [c for c in gate if topo.die(c) != topo.die(me)]
+    rest = [c for c in here if c not in gate and topo.die(c) != topo.die(me)]
+    jobs = {
+        near[0]: ("codes", ["M", "F1"]), near[1]: ("plane", ["M", "F1"]),
+        far[0]: ("codes", ["F2", "F3"]), far[1]: ("plane", ["F2", "F3"]),
+        rest[0]: ("plane", ["P1", "P2", "P3"]),
+    }
+    feeds = {"plane": [rest[0], near[1], far[1]], "codes": [near[0], far[0]]}
+    return kinds, jobs, feeds
+
+
+def _send(g, T, topo, src_core, dst_cores, src, dsts, sem):
+    mask = topo.mask(src_core, dst_cores[0])
+    for d in dst_cores:
+        mask &= topo.mask(src_core, d)
+    ids = [DstId(rid=topo.addr(d)[0], pnc=topo.addr(d)[1]) for d in dst_cores]
+    g.remote_dma_fused([RemoteDMATransfer(dst_ids=ids, dma_engine_mask=mask, remote_sem=sem, srcs=[src], dsts=dsts)],
+                       local_sem=T.sem.sent)
+    return bin(mask).count("1")
+
+
+def _slot(T, what, s):
+    if what == "codes":
+        return T.rq[:, 128 * s:128 * s + 128].bitcast(dt.uint8)
+    return T.rp[:, 128 * s:128 * s + 128]
+
+
+def _own(T, what):
+    return T.q[:].bitcast(dt.uint8) if what == "codes" else T.qp[:]
+
+
+def _helper(g, core, T, topo):
+    cores = list(T.cores)
+    home = [r for r in range(N) if topo.chip(cores[r]) == topo.chip(core)]
+    if not home:
+        return
+    r = home[0]
+    kinds, jobs, feeds = _plan(r, cores, topo)
+    if core not in jobs:
+        return
+    what, ks = jobs[core]
+    n_in = bin(topo.mask(cores[r], core)).count("1")
+    g.wait_ge(T.sem.feed, n_in)
+    n = _send(g, T, topo, core, [cores[kinds[k]] for k in ks], _own(T, what), [_slot(T, what, r) for k in ks],
+              T.sem["arr%d" % r])
+    g.wait_ge(T.sem.sent, n)
+
+
+def rank_program(g, core, T, topo):
+    rank = T.rank_of(core)
+    if rank is None:
+        _helper(g, core, T, topo)
+        return
+    cores = list(T.cores)
+    S = T.sem
+    v, te, sc, sy = g.vector, g.tensor, g.scalar, g.sync
+    kinds, jobs, feeds = _plan(rank, cores, topo)
+
+    sy.dma_start(T.b_sb[:], T.b[:]).then_inc(S.ld_b, 16)
+    sc.dma_start(T.a_sb[:, 0:1024], T.a[:, 0:1024]).then_inc(S.ld_a0, 16)
+    sy.dma_start(T.a_sb[:, 1024:2048], T.a[:, 1024:2048]).then_inc(S.ld_a1, 16)
+
+    v.memset(T.eye[:], 1.0).then_inc(S.c_ones, 1)
+    v.memset(T.diag[:], 0.0).then_inc(S.c_zero, 1)
+    g.wait_ge(S.c_ones, 1)
+    g.affine_select(T.eye[:], T.eye[:], [[-1, 128]], AluOpType.is_equal, 0.0, 0, 1).then_inc(S.c_eye, 1)
+    v.wait_ge(S.c_eye, 1)
+    v.wait_ge(S.c_zero, 1)
+    v.tensor_copy(T.diag[:, 3:515:4], T.eye[:]).then_inc(S.c_diag, 1)
+    v.wait_ge(S.c_diag, 1)
+    for i in range(4):
+        v.quantize_mx(T.wq[:, 128 * i:128 * i + 128], T.wp[:, 128 * i:128 * i + 128],
+                      T.diag[:, 3 - i:515 - i]).then_inc(S.w_done, 1)
+
+    v.wait_ge(S.ld_b, 16)
+    v.quantize_mx(T.bq[:], T.bp[:], T.b_sb[:]).then_inc(S.qb, 1)
+    v.wait_ge(S.ld_a0, 16)
+    v.quantize_mx(T.aq[:, 0:256], T.ap[:, 0:256], T.a_sb[:, 0:1024]).then_inc(S.qa, 1)
+    v.wait_ge(S.ld_a1, 16)
+    v.quantize_mx(T.aq[:, 256:512], T.ap[:, 256:512], T.a_sb[:, 1024:2048]).then_inc(S.qa, 1)
+
+    te.wait_ge(S.qb, 1)
+    for i in range(4):
+        if i % 2 == 0:
+            te.wait_ge(S.qa, i // 2 + 1)
+        te.matmul_mx(T.own[:, 512 * i:512 * i + 128], T.aq[:, 128 * i:128 * i + 128], T.ap[:, 128 * i:128 * i + 128],
+                     T.bq[:], T.bp[:], True, True).then_inc(S.mm, 1)
+    for i in range(4):
+        te.matmul_mx(T.acc[:, 512 * i:512 * i + 128], T.aq[:, 128 * i:128 * i + 128], T.ap[:, 128 * i:128 * i + 128],
+                     T.bq[:], T.bp[:], True, False)
+
+    for i in range(4):
+        if i % 2 == 0:
+            v.wait_ge(S.mm, i + 1)
+            v.tensor_copy(T.h_sb[:, i:512:4], T.own[:, 512 * i:512 * i + 128]).then_inc(S.hcp_v, 1)
+        else:
+            sc.wait_ge(S.mm, i + 1)
+            sc.activation(T.h_sb[:, i:512:4], T.own[:, 512 * i:512 * i + 128],
+                          ActivationFunctionType.Copy).then_inc(S.hcp_s, 1)
+    v.wait_ge(S.hcp_v, 2)
+    v.wait_ge(S.hcp_s, 2)
+    v.quantize_mx(T.q[:], T.qp[:], T.h_sb[:]).then_inc(S.q_done, 1)
+
+    g.wait_ge(S.q_done, 1)
+    n = 0
+    for what in ("plane", "codes"):
+        n += _send(g, T, topo, core, feeds[what], _own(T, what), [_own(T, what) for c in feeds[what]], S.feed)
+    ks = ["P1", "P2", "P3"]
+    n += _send(g, T, topo, core, [cores[kinds[k]] for k in ks], _own(T, "codes"), [_slot(T, "codes", rank) for k in ks],
+               S["arr%d" % rank])
+
+    src_of = {}
+    cnt_of = {}
+    for s in range(N):
+        if s == rank:
+            continue
+        ks_s, jobs_s, feeds_s = _plan(s, cores, topo)
+        for k in ks_s:
+            if ks_s[k] == rank:
+                src_of[k] = s
+        cnt_of[s] = 2 * bin(topo.mask(cores[s], core)).count("1")
+    te.wait_ge(S.w_done, 4)
+    for j, k in enumerate(TAKE):
+        s = src_of[k]
+        last = j == len(TAKE) - 1
+        te.wait_ge(S["arr%d" % s], cnt_of[s])
+        for i in range(4):
+            m = te.matmul_mx(T.acc[:, 512 * i:512 * i + 128], T.wq[:, 128 * i:128 * i + 128],
+                             T.wp[:, 128 * i:128 * i + 128], T.rq[:, 128 * s:128 * s + 128],
+                             T.rp[:, 128 * s:128 * s + 128], False, last)
+            if last:
+                m.then_inc(S.fin, 1)
+
+    for i in range(4):
+        if i % 2 == 0:
+            v.wait_ge(S.fin, i + 1)
+            v.tensor_copy(T.y_sb[:, i:512:4], T.acc[:, 512 * i:512 * i + 128]).then_inc(S.ycp_v, 1)
+        else:
+            sc.wait_ge(S.fin, i + 1)
+            sc.activation(T.y_sb[:, i:512:4], T.acc[:, 512 * i:512 * i + 128],
+                          ActivationFunctionType.Copy).then_inc(S.ycp_s, 1)
+    sy.wait_ge(S.ycp_v, 2)
+    sy.wait_ge(S.ycp_s, 2)
+    sy.dma_start(T.y[:], T.y_sb[:]).then_inc(S.stored, 16)
+    sy.wait_ge(S.stored, 16)
+    g.wait_ge(S.sent, n)

@@ -24,7 +24,7 @@ SCRATCH = {
     "acc": ("psum", [128, 2048], "float32"),
     "y_sb": ("sbuf", [128, 512], "float32"),
 }
-SEMAPHORES = ["ld_b", "ld_a0", "ld_a1", "c_ones", "c_zero", "c_eye", "c_diag", "w_done", "qb", "qa", "mm",
+SEMAPHORES = ["ld_b", "ld_a0", "ld_a1", "c_ones", "c_zero", "c_eye", "c_diag", "w_done", "w_arr", "qb", "qa", "mm",
               "hcp_v", "hcp_s", "q_done", "feed", "sent", "fin", "ycp_v", "ycp_s", "stored"] + ["arr%d" % s for s in range(N)]
 
 TAKE = ["P1", "P2", "P3", "M", "F2", "F1", "F3"]
@@ -48,24 +48,23 @@ def _plan(r, cores, topo):
     gate = [c for c in here if topo.may_write(c, cores[mate])]
     near = [c for c in gate if topo.die(c) == topo.die(me)]
     far = [c for c in gate if topo.die(c) != topo.die(me)]
-    rest = [c for c in here if c not in gate and topo.die(c) != topo.die(me)]
     jobs = {
-        near[0]: ("codes", ["M", "F1"]), near[1]: ("plane", ["M", "F1"]),
-        far[0]: ("codes", ["F2", "F3"]), far[1]: ("plane", ["F2", "F3"]),
-        rest[0]: ("plane", ["P1", "P2", "P3"]),
+        near[0]: ("codes", ["M", "F1"], 0), near[1]: ("plane", ["M", "F1"], 1),
+        far[0]: ("codes", ["F2", "F3"], 2), far[1]: ("plane", ["F2", "F3"], 3),
     }
-    feeds = {"plane": [rest[0], near[1], far[1]], "codes": [near[0], far[0]]}
-    return kinds, jobs, feeds
+    feeds = {"plane": [near[1], far[1]], "codes": [near[0], far[0]]}
+    out = topo.mask(me, cores[p[0]])
+    masks = {"peers": out, "feed": topo.mask(me, near[0]) & topo.mask(me, far[0]) & ~out}
+    return kinds, jobs, feeds, masks
 
 
-def _send(g, T, topo, src_core, dst_cores, src, dsts, sem):
-    mask = topo.mask(src_core, dst_cores[0])
-    for d in dst_cores:
-        mask &= topo.mask(src_core, d)
-    ids = [DstId(rid=topo.addr(d)[0], pnc=topo.addr(d)[1]) for d in dst_cores]
-    g.remote_dma_fused([RemoteDMATransfer(dst_ids=ids, dma_engine_mask=mask, remote_sem=sem, srcs=[src], dsts=dsts)],
-                       local_sem=T.sem.sent)
+def _bits(mask):
     return bin(mask).count("1")
+
+
+def _tr(topo, mask, dst_cores, src, dsts, sem):
+    ids = [DstId(rid=topo.addr(d)[0], pnc=topo.addr(d)[1]) for d in dst_cores]
+    return RemoteDMATransfer(dst_ids=ids, dma_engine_mask=mask, remote_sem=sem, srcs=[src], dsts=dsts)
 
 
 def _slot(T, what, s):
@@ -78,21 +77,44 @@ def _own(T, what):
     return T.q[:].bitcast(dt.uint8) if what == "codes" else T.qp[:]
 
 
+def _selection(g, T, which):
+    S, v = T.sem, g.vector
+    v.memset(T.eye[:], 1.0).then_inc(S.c_ones, 1)
+    v.memset(T.diag[:], 0.0).then_inc(S.c_zero, 1)
+    g.wait_ge(S.c_ones, 1)
+    g.affine_select(T.eye[:], T.eye[:], [[-1, 128]], AluOpType.is_equal, 0.0, 0, 1).then_inc(S.c_eye, 1)
+    v.wait_ge(S.c_eye, 1)
+    v.wait_ge(S.c_zero, 1)
+    v.tensor_copy(T.diag[:, 3:515:4], T.eye[:]).then_inc(S.c_diag, 1)
+    v.wait_ge(S.c_diag, 1)
+    for i in which:
+        v.quantize_mx(T.wq[:, 128 * i:128 * i + 128], T.wp[:, 128 * i:128 * i + 128],
+                      T.diag[:, 3 - i:515 - i]).then_inc(S.w_done, 1)
+
+
 def _helper(g, core, T, topo):
     cores = list(T.cores)
     home = [r for r in range(N) if topo.chip(cores[r]) == topo.chip(core)]
     if not home:
         return
     r = home[0]
-    kinds, jobs, feeds = _plan(r, cores, topo)
+    kinds, jobs, feeds, masks = _plan(r, cores, topo)
     if core not in jobs:
         return
-    what, ks = jobs[core]
-    n_in = bin(topo.mask(cores[r], core)).count("1")
-    g.wait_ge(T.sem.feed, n_in)
-    n = _send(g, T, topo, core, [cores[kinds[k]] for k in ks], _own(T, what), [_slot(T, what, r) for k in ks],
-              T.sem["arr%d" % r])
-    g.wait_ge(T.sem.sent, n)
+    what, ks, piece = jobs[core]
+    dst = [cores[kinds[k]] for k in ks]
+    mask = topo.mask(core, cores[r])
+    for d in dst:
+        mask &= topo.mask(core, d)
+    _selection(g, T, [0])
+    g.wait_ge(T.sem.w_done, 1)
+    lo, hi = 128 * piece // len(jobs), 128 * (piece + 1) // len(jobs)
+    for ap in (T.wq[:, lo:hi].bitcast(dt.uint8), T.wp[:, lo:hi]):
+        g.remote_dma_fused([_tr(topo, mask, [cores[r]], ap, [ap], T.sem.w_arr)], local_sem=T.sem.sent)
+    g.wait_ge(T.sem.feed, _bits(masks["feed"]))
+    g.remote_dma_fused([_tr(topo, mask, dst, _own(T, what), [_slot(T, what, r) for k in ks], T.sem["arr%d" % r])],
+                       local_sem=T.sem.sent)
+    g.wait_ge(T.sem.sent, 3 * _bits(mask))
 
 
 def rank_program(g, core, T, topo):
@@ -103,72 +125,67 @@ def rank_program(g, core, T, topo):
     cores = list(T.cores)
     S = T.sem
     v, te, sc, sy = g.vector, g.tensor, g.scalar, g.sync
-    kinds, jobs, feeds = _plan(rank, cores, topo)
+    kinds, jobs, feeds, masks = _plan(rank, cores, topo)
 
     sy.dma_start(T.b_sb[:], T.b[:]).then_inc(S.ld_b, 16)
     sc.dma_start(T.a_sb[:, 0:1024], T.a[:, 0:1024]).then_inc(S.ld_a0, 16)
     sy.dma_start(T.a_sb[:, 1024:2048], T.a[:, 1024:2048]).then_inc(S.ld_a1, 16)
 
-    v.memset(T.eye[:], 1.0).then_inc(S.c_ones, 1)
-    v.memset(T.diag[:], 0.0).then_inc(S.c_zero, 1)
-    g.wait_ge(S.c_ones, 1)
-    g.affine_select(T.eye[:], T.eye[:], [[-1, 128]], AluOpType.is_equal, 0.0, 0, 1).then_inc(S.c_eye, 1)
-    v.wait_ge(S.c_eye, 1)
-    v.wait_ge(S.c_zero, 1)
-    v.tensor_copy(T.diag[:, 3:515:4], T.eye[:]).then_inc(S.c_diag, 1)
-    v.wait_ge(S.c_diag, 1)
-    for i in range(4):
-        v.quantize_mx(T.wq[:, 128 * i:128 * i + 128], T.wp[:, 128 * i:128 * i + 128],
-                      T.diag[:, 3 - i:515 - i]).then_inc(S.w_done, 1)
+    _selection(g, T, [1, 2, 3])
 
     v.wait_ge(S.ld_b, 16)
     v.quantize_mx(T.bq[:], T.bp[:], T.b_sb[:]).then_inc(S.qb, 1)
-    v.wait_ge(S.ld_a0, 16)
-    v.quantize_mx(T.aq[:, 0:256], T.ap[:, 0:256], T.a_sb[:, 0:1024]).then_inc(S.qa, 1)
-    v.wait_ge(S.ld_a1, 16)
-    v.quantize_mx(T.aq[:, 256:512], T.ap[:, 256:512], T.a_sb[:, 1024:2048]).then_inc(S.qa, 1)
+    for i in range(4):
+        if i == 0:
+            v.wait_ge(S.ld_a0, 16)
+        if i == 2:
+            v.wait_ge(S.ld_a1, 16)
+        v.quantize_mx(T.aq[:, 128 * i:128 * i + 128], T.ap[:, 128 * i:128 * i + 128],
+                      T.a_sb[:, 512 * i:512 * i + 512]).then_inc(S.qa, 1)
 
     te.wait_ge(S.qb, 1)
     for i in range(4):
-        if i % 2 == 0:
-            te.wait_ge(S.qa, i // 2 + 1)
+        te.wait_ge(S.qa, i + 1)
         te.matmul_mx(T.own[:, 512 * i:512 * i + 128], T.aq[:, 128 * i:128 * i + 128], T.ap[:, 128 * i:128 * i + 128],
                      T.bq[:], T.bp[:], True, True).then_inc(S.mm, 1)
     for i in range(4):
         te.matmul_mx(T.acc[:, 512 * i:512 * i + 128], T.aq[:, 128 * i:128 * i + 128], T.ap[:, 128 * i:128 * i + 128],
                      T.bq[:], T.bp[:], True, False)
 
-    for i in range(4):
-        if i % 2 == 0:
-            v.wait_ge(S.mm, i + 1)
-            v.tensor_copy(T.h_sb[:, i:512:4], T.own[:, 512 * i:512 * i + 128]).then_inc(S.hcp_v, 1)
-        else:
-            sc.wait_ge(S.mm, i + 1)
-            sc.activation(T.h_sb[:, i:512:4], T.own[:, 512 * i:512 * i + 128],
-                          ActivationFunctionType.Copy).then_inc(S.hcp_s, 1)
-    v.wait_ge(S.hcp_v, 2)
-    v.wait_ge(S.hcp_s, 2)
+    for i in (0, 1, 2):
+        sc.wait_ge(S.mm, i + 1)
+        sc.activation(T.h_sb[:, i:512:4], T.own[:, 512 * i:512 * i + 128],
+                      ActivationFunctionType.Copy).then_inc(S.hcp_s, 1)
+    v.wait_ge(S.mm, 4)
+    v.tensor_copy(T.h_sb[:, 3:512:4], T.own[:, 1536:1664]).then_inc(S.hcp_v, 1)
+    v.wait_ge(S.hcp_v, 1)
+    v.wait_ge(S.hcp_s, 3)
     v.quantize_mx(T.q[:], T.qp[:], T.h_sb[:]).then_inc(S.q_done, 1)
 
     g.wait_ge(S.q_done, 1)
     n = 0
-    for what in ("plane", "codes"):
-        n += _send(g, T, topo, core, feeds[what], _own(T, what), [_own(T, what) for c in feeds[what]], S.feed)
-    ks = ["P1", "P2", "P3"]
-    n += _send(g, T, topo, core, [cores[kinds[k]] for k in ks], _own(T, "codes"), [_slot(T, "codes", rank) for k in ks],
-               S["arr%d" % rank])
+    arr = S["arr%d" % rank]
+    for what, ks, fed in (("codes", ["P1"], True), ("plane", ["P1", "P2", "P3"], True), ("codes", ["P2", "P3"], False)):
+        trs = [_tr(topo, masks["peers"], [cores[kinds[k]] for k in ks], _own(T, what),
+                   [_slot(T, what, rank) for k in ks], arr)]
+        n += _bits(masks["peers"])
+        if fed:
+            trs.append(_tr(topo, masks["feed"], feeds[what], _own(T, what), [_own(T, what) for c in feeds[what]], S.feed))
+            n += _bits(masks["feed"])
+        g.remote_dma_fused(trs, local_sem=S.sent)
 
     src_of = {}
     cnt_of = {}
     for s in range(N):
         if s == rank:
             continue
-        ks_s, jobs_s, feeds_s = _plan(s, cores, topo)
+        ks_s = _plan(s, cores, topo)[0]
         for k in ks_s:
             if ks_s[k] == rank:
                 src_of[k] = s
-        cnt_of[s] = 2 * bin(topo.mask(cores[s], core)).count("1")
-    te.wait_ge(S.w_done, 4)
+        cnt_of[s] = 2 * _bits(topo.mask(cores[s], core))
+    te.wait_ge(S.w_done, 3)
+    te.wait_ge(S.w_arr, 2 * len(jobs) * _bits(masks["peers"]))
     for j, k in enumerate(TAKE):
         s = src_of[k]
         last = j == len(TAKE) - 1

@@ -15,6 +15,8 @@ SCRATCH = {
     "diag": ("sbuf", [128, 516], "bfloat16"),
     "wq": ("sbuf", [128, 512], "float8_e4m3fn_x4"),
     "wp": ("sbuf", [128, 512], "uint8"),
+    "vq": ("sbuf", [128, 128], "float8_e4m3fn_x4"),
+    "vp": ("sbuf", [128, 128], "uint8"),
     "h_sb": ("sbuf", [128, 512], "bfloat16"),
     "q": ("sbuf", [128, 128], "float8_e4m3fn_x4"),
     "qp": ("sbuf", [128, 128], "uint8"),
@@ -24,10 +26,12 @@ SCRATCH = {
     "acc": ("psum", [128, 2048], "float32"),
     "y_sb": ("sbuf", [128, 512], "float32"),
 }
-SEMAPHORES = ["ld_b", "ld_a0", "ld_a1", "c_ones", "c_zero", "c_eye", "c_diag", "w_done", "w_arr", "qb", "qa", "mm",
-              "hcp_v", "hcp_s", "q_done", "feed", "sent", "fin", "ycp_v", "ycp_s", "stored"] + ["arr%d" % s for s in range(N)]
+SEMAPHORES = ["ld_b", "ld_a0", "ld_a1", "c_ones", "c_zero", "c_eye", "c_diag", "w_done", "w_arr", "v_done", "w_feed",
+              "qb", "qa", "mm", "hcp_v", "hcp_s", "q_done", "feed", "sent", "fin", "ycp_v", "ycp_s",
+              "stored"] + ["arr%d" % s for s in range(N)]
 
 TAKE = ["P1", "P2", "P3", "M", "F2", "F1", "F3"]
+W_HELP = 96
 
 
 def _rot(lst, x):
@@ -58,6 +62,17 @@ def _plan(r, cores, topo):
     return kinds, jobs, feeds, masks
 
 
+def _relay(feeds):
+    return feeds["plane"][0]
+
+
+def _hmask(topo, core, cores, r, kinds):
+    mask = topo.mask(core, cores[r])
+    for k in kinds:
+        mask &= topo.mask(core, cores[kinds[k]])
+    return mask
+
+
 def _bits(mask):
     return bin(mask).count("1")
 
@@ -77,7 +92,7 @@ def _own(T, what):
     return T.q[:].bitcast(dt.uint8) if what == "codes" else T.qp[:]
 
 
-def _selection(g, T, which):
+def _selection(g, T, which, share=False):
     S, v = T.sem, g.vector
     v.memset(T.eye[:], 1.0).then_inc(S.c_ones, 1)
     v.memset(T.diag[:], 0.0).then_inc(S.c_zero, 1)
@@ -87,6 +102,8 @@ def _selection(g, T, which):
     v.wait_ge(S.c_zero, 1)
     v.tensor_copy(T.diag[:, 3:515:4], T.eye[:]).then_inc(S.c_diag, 1)
     v.wait_ge(S.c_diag, 1)
+    if share:
+        v.quantize_mx(T.vq[:], T.vp[:], T.diag[:, 3:515]).then_inc(S.v_done, 1)
     for i in which:
         v.quantize_mx(T.wq[:, 128 * i:128 * i + 128], T.wp[:, 128 * i:128 * i + 128],
                       T.diag[:, 3 - i:515 - i]).then_inc(S.w_done, 1)
@@ -103,18 +120,22 @@ def _helper(g, core, T, topo):
         return
     what, ks, piece = jobs[core]
     dst = [cores[kinds[k]] for k in ks]
-    mask = topo.mask(core, cores[r])
-    for d in dst:
-        mask &= topo.mask(core, d)
+    mask = _hmask(topo, core, cores, r, kinds)
+    calls = 3
     _selection(g, T, [0])
     g.wait_ge(T.sem.w_done, 1)
-    lo, hi = 128 * piece // len(jobs), 128 * (piece + 1) // len(jobs)
+    lo, hi = W_HELP * piece // len(jobs), W_HELP * (piece + 1) // len(jobs)
     for ap in (T.wq[:, lo:hi].bitcast(dt.uint8), T.wp[:, lo:hi]):
         g.remote_dma_fused([_tr(topo, mask, [cores[r]], ap, [ap], T.sem.w_arr)], local_sem=T.sem.sent)
+    if core == _relay(feeds):
+        g.wait_ge(T.sem.w_feed, _bits(masks["feed"]))
+        g.remote_dma_fused([_tr(topo, mask, [cores[kinds["P1"]]], T.vp[:, W_HELP:128], [T.wp[:, W_HELP:128]],
+                                T.sem.w_arr)], local_sem=T.sem.sent)
+        calls += 1
     g.wait_ge(T.sem.feed, _bits(masks["feed"]))
     g.remote_dma_fused([_tr(topo, mask, dst, _own(T, what), [_slot(T, what, r) for k in ks], T.sem["arr%d" % r])],
                        local_sem=T.sem.sent)
-    g.wait_ge(T.sem.sent, 3 * _bits(mask))
+    g.wait_ge(T.sem.sent, calls * _bits(mask))
 
 
 def rank_program(g, core, T, topo):
@@ -131,7 +152,13 @@ def rank_program(g, core, T, topo):
     sc.dma_start(T.a_sb[:, 0:1024], T.a[:, 0:1024]).then_inc(S.ld_a0, 16)
     sy.dma_start(T.a_sb[:, 1024:2048], T.a[:, 1024:2048]).then_inc(S.ld_a1, 16)
 
-    _selection(g, T, [1, 2, 3])
+    _selection(g, T, [1, 2, 3], share=True)
+
+    g.wait_ge(S.v_done, 1)
+    g.remote_dma_fused([_tr(topo, masks["peers"], [cores[kinds["P1"]]], T.vq[:, W_HELP:128].bitcast(dt.uint8),
+                            [T.wq[:, W_HELP:128].bitcast(dt.uint8)], S.w_arr)], local_sem=S.sent)
+    g.remote_dma_fused([_tr(topo, masks["feed"], [_relay(feeds)], T.vp[:, W_HELP:128], [T.vp[:, W_HELP:128]],
+                            S.w_feed)], local_sem=S.sent)
 
     v.wait_ge(S.ld_b, 16)
     v.quantize_mx(T.bq[:], T.bp[:], T.b_sb[:]).then_inc(S.qb, 1)
@@ -163,7 +190,7 @@ def rank_program(g, core, T, topo):
     v.quantize_mx(T.q[:], T.qp[:], T.h_sb[:]).then_inc(S.q_done, 1)
 
     g.wait_ge(S.q_done, 1)
-    n = 0
+    n = _bits(masks["peers"]) + _bits(masks["feed"])
     arr = S["arr%d" % rank]
     for what, ks, fed in (("codes", ["P1"], True), ("plane", ["P1", "P2", "P3"], True), ("codes", ["P2", "P3"], False)):
         trs = [_tr(topo, masks["peers"], [cores[kinds[k]] for k in ks], _own(T, what),
@@ -184,13 +211,18 @@ def rank_program(g, core, T, topo):
             if ks_s[k] == rank:
                 src_of[k] = s
         cnt_of[s] = 2 * _bits(topo.mask(cores[s], core))
+    pre = src_of["P1"]
+    kinds_p, jobs_p, feeds_p, masks_p = _plan(pre, cores, topo)
+    w_all = sum(2 * _bits(_hmask(topo, c, cores, rank, kinds)) for c in jobs)
+    w_all += _bits(masks_p["peers"]) + _bits(_hmask(topo, _relay(feeds_p), cores, pre, kinds_p))
     te.wait_ge(S.w_done, 3)
-    te.wait_ge(S.w_arr, 2 * len(jobs) * _bits(masks["peers"]))
     for j, k in enumerate(TAKE):
         s = src_of[k]
         last = j == len(TAKE) - 1
         te.wait_ge(S["arr%d" % s], cnt_of[s])
-        for i in range(4):
+        for i in ((1, 2, 3, 0) if j == 0 else (0, 1, 2, 3)):
+            if j == 0 and i == 0:
+                te.wait_ge(S.w_arr, w_all)
             m = te.matmul_mx(T.acc[:, 512 * i:512 * i + 128], T.wq[:, 128 * i:128 * i + 128],
                              T.wp[:, 128 * i:128 * i + 128], T.rq[:, 128 * s:128 * s + 128],
                              T.rp[:, 128 * s:128 * s + 128], False, last)

from concourse.bass import DstId, RemoteDMATransfer
from concourse.mybir import dt, AluOpType, ActivationFunctionType

N = 8
SIM_CORES = 128

SCRATCH = {
    "a_sb": ("sbuf", [128, 2048], "bfloat16"),
    "b_sb": ("sbuf", [128, 512], "bfloat16"),
    "aq": ("sbuf", [128, 512], "float8_e4m3fn_x4"),
    "ap": ("sbuf", [128, 512], "uint8"),
    "bq": ("sbuf", [128, 128], "float8_e4m3fn_x4"),
    "bp": ("sbuf", [128, 128], "uint8"),
    "eye": ("sbuf", [128, 128], "bfloat16"),
    "diag": ("sbuf", [128, 516], "bfloat16"),
    "wq": ("sbuf", [128, 512], "float8_e4m3fn_x4"),
    "wp": ("sbuf", [128, 512], "uint8"),
    "vq": ("sbuf", [128, 128], "float8_e4m3fn_x4"),
    "vp": ("sbuf", [128, 128], "uint8"),
    "h_sb": ("sbuf", [128, 512], "bfloat16"),
    "q": ("sbuf", [128, 128], "float8_e4m3fn_x4"),
    "qp": ("sbuf", [128, 128], "uint8"),
    "rq": ("sbuf", [128, 128 * N], "float8_e4m3fn_x4"),
    "rp": ("sbuf", [128, 128 * N], "uint8"),
    "own": ("psum", [128, 2048], "float32"),
    "acc": ("psum", [128, 2048], "float32"),
    "y_sb": ("sbuf", [128, 512], "float32"),
}
SEMAPHORES = ["ld_b", "ld_a0", "ld_a1", "c_ones", "c_zero", "c_eye", "c_diag", "w_done", "w_arr", "v_done", "w_feed",
              "qb", "qa", "mm", "hcp_v", "hcp_s", "q_done", "feed", "sent", "fin", "ycp_v", "ycp_s",
              "stored"] + ["arr%d" % s for s in range(N)]

TAKE = ["P1", "P2", "P3", "M", "F2", "F1", "F3"]
W_HELP = 96


def _rot(lst, x):
    k = lst.index(x)
    return lst[k + 1:] + lst[:k]


def _plan(r, cores, topo):
    me = cores[r]
    ch = [topo.chip(c) for c in cores]
    plane = [s for s in range(N) if s == r or topo.same_plane(ch[s], ch[r])]
    mate = [s for s in range(N) if topo.mates(ch[s], ch[r])][0]
    other = [s for s in range(N) if s == mate or topo.same_plane(ch[s], ch[mate])]
    p = _rot(plane, r)
    f = _rot(other, mate)
    kinds = {"P1": p[0], "P2": p[1], "P3": p[2], "M": mate, "F1": f[0], "F2": f[1], "F3": f[2]}
    here = [c for c in range(SIM_CORES) if topo.chip(c) == ch[r] and c != me]
    gate = [c for c in here if topo.may_write(c, cores[mate])]
    near = [c for c in gate if topo.die(c) == topo.die(me)]
    far = [c for c in gate if topo.die(c) != topo.die(me)]
    jobs = {
        near[0]: ("codes", ["M", "F1"], 0), near[1]: ("plane", ["M", "F1"], 1),
        far[0]: ("codes", ["F2", "F3"], 2), far[1]: ("plane", ["F2", "F3"], 3),
    }
    feeds = {"plane": [near[1], far[1]], "codes": [near[0], far[0]]}
    out = topo.mask(me, cores[p[0]])
    masks = {"peers": out, "feed": topo.mask(me, near[0]) & topo.mask(me, far[0]) & ~out}
    return kinds, jobs, feeds, masks


def _relay(feeds):
    return feeds["plane"][0]


def _hmask(topo, core, cores, r, kinds):
    mask = topo.mask(core, cores[r])
    for k in kinds:
        mask &= topo.mask(core, cores[kinds[k]])
    return mask


def _bits(mask):
    return bin(mask).count("1")


def _tr(topo, mask, dst_cores, src, dsts, sem):
    ids = [DstId(rid=topo.addr(d)[0], pnc=topo.addr(d)[1]) for d in dst_cores]
    return RemoteDMATransfer(dst_ids=ids, dma_engine_mask=mask, remote_sem=sem, srcs=[src], dsts=dsts)


def _slot(T, what, s):
    if what == "codes":
        return T.rq[:, 128 * s:128 * s + 128].bitcast(dt.uint8)
    return T.rp[:, 128 * s:128 * s + 128]


def _own(T, what):
    return T.q[:].bitcast(dt.uint8) if what == "codes" else T.qp[:]


def _selection(g, T, which, share=False):
    S, v = T.sem, g.vector
    v.memset(T.eye[:], 1.0).then_inc(S.c_ones, 1)
    v.memset(T.diag[:], 0.0).then_inc(S.c_zero, 1)
    g.wait_ge(S.c_ones, 1)
    g.affine_select(T.eye[:], T.eye[:], [[-1, 128]], AluOpType.is_equal, 0.0, 0, 1).then_inc(S.c_eye, 1)
    v.wait_ge(S.c_eye, 1)
    v.wait_ge(S.c_zero, 1)
    v.tensor_copy(T.diag[:, 3:515:4], T.eye[:]).then_inc(S.c_diag, 1)
    v.wait_ge(S.c_diag, 1)
    if share:
        v.quantize_mx(T.vq[:], T.vp[:], T.diag[:, 3:515]).then_inc(S.v_done, 1)
    for i in which:
        v.quantize_mx(T.wq[:, 128 * i:128 * i + 128], T.wp[:, 128 * i:128 * i + 128],
                      T.diag[:, 3 - i:515 - i]).then_inc(S.w_done, 1)


def _helper(g, core, T, topo):
    cores = list(T.cores)
    home = [r for r in range(N) if topo.chip(cores[r]) == topo.chip(core)]
    if not home:
        return
    r = home[0]
    kinds, jobs, feeds, masks = _plan(r, cores, topo)
    if core not in jobs:
        return
    what, ks, piece = jobs[core]
    dst = [cores[kinds[k]] for k in ks]
    mask = _hmask(topo, core, cores, r, kinds)
    calls = 3
    _selection(g, T, [0])
    g.wait_ge(T.sem.w_done, 1)
    lo, hi = W_HELP * piece // len(jobs), W_HELP * (piece + 1) // len(jobs)
    for ap in (T.wq[:, lo:hi].bitcast(dt.uint8), T.wp[:, lo:hi]):
        g.remote_dma_fused([_tr(topo, mask, [cores[r]], ap, [ap], T.sem.w_arr)], local_sem=T.sem.sent)
    if core == _relay(feeds):
        g.wait_ge(T.sem.w_feed, _bits(masks["feed"]))
        g.remote_dma_fused([_tr(topo, mask, [cores[kinds["P1"]]], T.vp[:, W_HELP:128], [T.wp[:, W_HELP:128]],
                                T.sem.w_arr)], local_sem=T.sem.sent)
        calls += 1
    g.wait_ge(T.sem.feed, _bits(masks["feed"]))
    g.remote_dma_fused([_tr(topo, mask, dst, _own(T, what), [_slot(T, what, r) for k in ks], T.sem["arr%d" % r])],
                       local_sem=T.sem.sent)
    g.wait_ge(T.sem.sent, calls * _bits(mask))


def rank_program(g, core, T, topo):
    rank = T.rank_of(core)
    if rank is None:
        _helper(g, core, T, topo)
        return
    cores = list(T.cores)
    S = T.sem
    v, te, sc, sy = g.vector, g.tensor, g.scalar, g.sync
    kinds, jobs, feeds, masks = _plan(rank, cores, topo)

    sy.dma_start(T.b_sb[:], T.b[:]).then_inc(S.ld_b, 16)
    sc.dma_start(T.a_sb[:, 0:1024], T.a[:, 0:1024]).then_inc(S.ld_a0, 16)
    sy.dma_start(T.a_sb[:, 1024:2048], T.a[:, 1024:2048]).then_inc(S.ld_a1, 16)

    _selection(g, T, [1, 2, 3], share=True)

    g.wait_ge(S.v_done, 1)
    g.remote_dma_fused([_tr(topo, masks["peers"], [cores[kinds["P1"]]], T.vq[:, W_HELP:128].bitcast(dt.uint8),
                            [T.wq[:, W_HELP:128].bitcast(dt.uint8)], S.w_arr)], local_sem=S.sent)
    g.remote_dma_fused([_tr(topo, masks["feed"], [_relay(feeds)], T.vp[:, W_HELP:128], [T.vp[:, W_HELP:128]],
                            S.w_feed)], local_sem=S.sent)

    v.wait_ge(S.ld_b, 16)
    v.quantize_mx(T.bq[:], T.bp[:], T.b_sb[:]).then_inc(S.qb, 1)
    for i in range(4):
        if i == 0:
            v.wait_ge(S.ld_a0, 16)
        if i == 2:
            v.wait_ge(S.ld_a1, 16)
        v.quantize_mx(T.aq[:, 128 * i:128 * i + 128], T.ap[:, 128 * i:128 * i + 128],
                      T.a_sb[:, 512 * i:512 * i + 512]).then_inc(S.qa, 1)

    te.wait_ge(S.qb, 1)
    for i in range(4):
        te.wait_ge(S.qa, i + 1)
        te.matmul_mx(T.own[:, 512 * i:512 * i + 128], T.aq[:, 128 * i:128 * i + 128], T.ap[:, 128 * i:128 * i + 128],
                     T.bq[:], T.bp[:], True, True).then_inc(S.mm, 1)
    for i in range(4):
        te.matmul_mx(T.acc[:, 512 * i:512 * i + 128], T.aq[:, 128 * i:128 * i + 128], T.ap[:, 128 * i:128 * i + 128],
                     T.bq[:], T.bp[:], True, False)

    for i in (0, 1, 2):
        sc.wait_ge(S.mm, i + 1)
        sc.activation(T.h_sb[:, i:512:4], T.own[:, 512 * i:512 * i + 128],
                      ActivationFunctionType.Copy).then_inc(S.hcp_s, 1)
    v.wait_ge(S.mm, 4)
    v.tensor_copy(T.h_sb[:, 3:512:4], T.own[:, 1536:1664]).then_inc(S.hcp_v, 1)
    v.wait_ge(S.hcp_v, 1)
    v.wait_ge(S.hcp_s, 3)
    v.quantize_mx(T.q[:], T.qp[:], T.h_sb[:]).then_inc(S.q_done, 1)

    g.wait_ge(S.q_done, 1)
    n = _bits(masks["peers"]) + _bits(masks["feed"])
    arr = S["arr%d" % rank]
    for what, ks, fed in (("codes", ["P1"], True), ("plane", ["P1", "P2", "P3"], True), ("codes", ["P2", "P3"], False)):
        trs = [_tr(topo, masks["peers"], [cores[kinds[k]] for k in ks], _own(T, what),
                   [_slot(T, what, rank) for k in ks], arr)]
        n += _bits(masks["peers"])
        if fed:
            trs.append(_tr(topo, masks["feed"], feeds[what], _own(T, what), [_own(T, what) for c in feeds[what]], S.feed))
            n += _bits(masks["feed"])
        g.remote_dma_fused(trs, local_sem=S.sent)

    src_of = {}
    cnt_of = {}
    for s in range(N):
        if s == rank:
            continue
        ks_s = _plan(s, cores, topo)[0]
        for k in ks_s:
            if ks_s[k] == rank:
                src_of[k] = s
        cnt_of[s] = 2 * _bits(topo.mask(cores[s], core))
    pre = src_of["P1"]
    kinds_p, jobs_p, feeds_p, masks_p = _plan(pre, cores, topo)
    w_all = sum(2 * _bits(_hmask(topo, c, cores, rank, kinds)) for c in jobs)
    w_all += _bits(masks_p["peers"]) + _bits(_hmask(topo, _relay(feeds_p), cores, pre, kinds_p))
    te.wait_ge(S.w_done, 3)
    for j, k in enumerate(TAKE):
        s = src_of[k]
        last = j == len(TAKE) - 1
        te.wait_ge(S["arr%d" % s], cnt_of[s])
        for i in ((1, 2, 3, 0) if j == 0 else (0, 1, 2, 3)):
            if j == 0 and i == 0:
                te.wait_ge(S.w_arr, w_all)
            m = te.matmul_mx(T.acc[:, 512 * i:512 * i + 128], T.wq[:, 128 * i:128 * i + 128],
                             T.wp[:, 128 * i:128 * i + 128], T.rq[:, 128 * s:128 * s + 128],
                             T.rp[:, 128 * s:128 * s + 128], False, last)
            if last:
                m.then_inc(S.fin, 1)

    for i in range(4):
        if i % 2 == 0:
            v.wait_ge(S.fin, i + 1)
            v.tensor_copy(T.y_sb[:, i:512:4], T.acc[:, 512 * i:512 * i + 128]).then_inc(S.ycp_v, 1)
        else:
            sc.wait_ge(S.fin, i + 1)
            sc.activation(T.y_sb[:, i:512:4], T.acc[:, 512 * i:512 * i + 128],
                          ActivationFunctionType.Copy).then_inc(S.ycp_s, 1)
    sy.wait_ge(S.ycp_v, 2)
    sy.wait_ge(S.ycp_s, 2)
    sy.dma_start(T.y[:], T.y_sb[:]).then_inc(S.stored, 16)
    sy.wait_ge(S.stored, 16)
    g.wait_ge(S.sent, n)
